import numpy as np
import ml_dtypes


def mxq(x, axis, fmt="e4m3"):
    dtype, down = {"e4m3": (ml_dtypes.float8_e4m3fn, 7), "e5m2": (ml_dtypes.float8_e5m2, 14)}[fmt]
    v = np.moveaxis(np.asarray(x, np.float32).astype(ml_dtypes.bfloat16).astype(np.float64), axis, -1)
    blocks = v.reshape(v.shape[:-1] + (-1, 32))
    amax = np.abs(blocks).max(-1, keepdims=True)
    byte = np.maximum(np.where(amax > 0, np.frexp(amax)[1] - 1 + 127, 0) - down, 1)
    scale = np.exp2(byte - 127.0)
    codes = (blocks / scale).astype(np.float32).astype(dtype).astype(np.float64)
    return np.moveaxis((codes * scale).reshape(v.shape), -1, axis)


WIDE = False


def mx_kscale(k):
    if not WIDE:
        return np.ones(k)
    levels = np.array([10, -10, 5, -5, 0])
    if k % 512:
        return np.exp2(np.random.permutation(np.resize(levels, k // 32))).repeat(32)
    a = np.empty((k // 512, 16))
    for p in range(k // 512):
        a[p, :8] = np.random.permutation(np.resize(levels, 8))
        for g in range(8):
            far = levels[np.abs(levels - a[p, g]) >= 10]
            a[p, g + 8] = far[np.random.randint(len(far))]
    return np.exp2(a.ravel()).repeat(32)


def f64(x):
    return np.asarray(x).astype(np.float64)


def striped(idx):
    return np.tile(idx.reshape(-1, 16).T, (8, 1)).astype(np.uint16)


def unstriped(offs):
    return offs[:16].T.reshape(-1).astype(np.int64)


def pack_weight(w):
    k, n = w.shape
    w = f64(np.asarray(w, np.float32).astype(ml_dtypes.bfloat16)).reshape(k // 32, 32, n)
    amax = np.abs(w).max(1)
    byte = np.clip(np.where(amax > 0, np.frexp(amax)[1] - 1 + 127 - 7, 1), 1, 254)
    scaled = (w * np.exp2(127.0 - byte)[:, None, :]).reshape(k, n).astype(np.float32)
    words = np.ascontiguousarray(scaled.reshape(k // 512, 128, 4, n).transpose(0, 1, 3, 2)).astype(ml_dtypes.float8_e4m3fn).view(np.uint8)
    return words, np.ascontiguousarray(byte.astype(np.uint8).reshape(k // 512, 16, n))


def unpack_weight(words, scales):
    g, p, n, _ = words.shape
    vals = np.ascontiguousarray(words).view(ml_dtypes.float8_e4m3fn).astype(np.float64) * np.repeat(np.exp2(scales.astype(np.float64) - 127.0), 8, axis=1)[..., None]
    return vals.transpose(0, 1, 3, 2).reshape(g * 512, n)


K, T, S, N = 512, 2048, 512, 128


def setup_inputs():
    n = np.random.standard_normal
    s = mx_kscale(K)[:, None]
    packed_xT = pack_weight(n((K, T)) * s)
    return {
        "x_words": packed_xT[0],
        "x_scales": packed_xT[1],
        "w1": (n((K, N)) / np.sqrt(K) / s).astype(np.float32),
        "alpha": (-np.random.uniform(0.5, 0.98, (N, 1))).astype(np.float32),
        "offs": striped(np.random.permutation(T)[:S]),
    }


def reference(x_words, x_scales, w1, alpha, offs):
    xq = unpack_weight(x_words, x_scales)[:, unstriped(offs)]
    y = mxq(f64(w1), 0, "e4m3").T @ xq
    en = np.exp(y)
    smo = 0.4 * en + 0.3 * (np.pad(en, ((0, 0), (1, 0)))[:, :S]) + 0.2 * (np.pad(en, ((0, 0), (2, 0)))[:, :S]) + 0.1 * (np.pad(en, ((0, 0), (3, 0)))[:, :S])
    agc = en * (np.exp(f64(alpha) * np.log(smo + 0.05)))
    return np.sqrt(agc + 2.0)

@@ -1,0 +1,85 @@
+from contextlib import ExitStack
+
+import concourse.mybir as mybir
+
+K, T, S, N = 512, 2048, 512, 128
+FLOPS = 2 * K * S * N
+
+F32 = mybir.dt.float32
+BF16 = mybir.dt.bfloat16
+I32 = mybir.dt.int32
+U32 = mybir.dt.uint32
+U16 = mybir.dt.uint16
+U8 = mybir.dt.uint8
+FP8X4 = mybir.dt.float8_e4m3fn_x4
+ACT = mybir.ActivationFunctionType
+ALU = mybir.AluOpType
+
+P = 128
+PAD = 8
+CHUNK = 256
+OUT_CHUNK = 256
+
+
+def tile_picked_ypcen_root_p_kernel(tc, x_words, x_scales, w1, alpha, offs, out):
+    nc = tc.nc
+    with ExitStack() as ctx:
+        sb = ctx.enter_context(tc.tile_pool(name="sb", bufs=1))
+        ps = ctx.enter_context(tc.psum_pool(name="ps", bufs=1))
+
+        offsets = sb.tile([P, S // 16], U16, name="offsets")
+        nc.sync.dma_start(offsets[:], offs)
+
+        scale_table = sb.tile([P, T], U8, name="scale_table", align_bytes=64)
+        nc.vector.memset(scale_table[:].bitcast(I32), 0)
+        for r in range(4):
+            nc.scalar.dma_start(scale_table[r:P:32, :].bitcast(I32), x_scales[0, r:16:4, :].bitcast(I32))
+
+        w_raw = sb.tile([P, 4, N], F32, name="w_raw")
+        nc.sync.dma_start(w_raw[:], w1.rearrange("(p j) m -> p j m", j=4))
+        word_table = sb.tile([P, T], U32, name="word_table", align_bytes=64)
+        nc.sync.dma_start(word_table[:].bitcast(I32), x_words[0].rearrange("p c r -> p (c r)").bitcast(I32))
+        alpha_col = sb.tile([P, 1], F32, name="alpha_col")
+        nc.scalar.dma_start(alpha_col[:], alpha)
+
+        w_bf = sb.tile([P, N, 4], BF16, name="w_bf", align_bytes=64)
+        nc.scalar.activation(out=w_bf[:], in_=w_raw[:].rearrange("p j m -> p m j"), func=ACT.Copy)
+        w_codes = sb.tile([P, N], U32, name="w_codes", align_bytes=64)
+        w_scales = sb.tile([P, N], U8, name="w_scales", align_bytes=64)
+        nc.vector.quantize_mx(out=w_codes[:].bitcast(FP8X4), scales=w_scales[:], in_=w_bf[:].rearrange("p m j -> p (m j)"))
+
+        x_sc = sb.tile([P, S], U8, name="x_sc", align_bytes=64)
+        nc.vector.tensor_copy(x_sc[:], scale_table[:].indirect(offsets[:]))
+
+        en = sb.tile([P, PAD + S], F32, name="en")
+        nc.vector.memset(en[:, 0:PAD], 0.0)
+        pair = sb.tile([P, PAD + S], F32, name="pair")
+        quad = sb.tile([P, S], F32, name="quad")
+        smo10 = sb.tile([P, S], F32, name="smo10")
+        x_codes = sb.tile([P, S], U32, name="x_codes", align_bytes=64)
+        for c0 in range(0, S, CHUNK):
+            c1 = c0 + CHUNK
+            nc.vector.tensor_copy(x_codes[:, c0:c1], word_table[:].indirect(offsets[:, c0 // 16 : c1 // 16]))
+            y = ps.tile([P, CHUNK], F32, name="y%d" % c0)
+            nc.tensor.matmul_mx(out=y[:], lhsT=w_codes[:].bitcast(FP8X4), lhsT_scale=w_scales[:],
+                                rhs=x_codes[:, c0:c1].bitcast(FP8X4), rhs_scale=x_sc[:, c0:c1], start=True, stop=True)
+            nc.scalar.activation(out=en[:, PAD + c0 : PAD + c1], in_=y[:], func=ACT.Exp)
+        for c0 in range(0, S, CHUNK):
+            c1 = c0 + CHUNK
+            lo = PAD + c0 - (2 if c0 == 0 else 0)
+            hi = PAD + c1
+            nc.vector.scalar_tensor_tensor(pair[:, lo:hi], en[:, lo:hi], 2.0, en[:, lo - 1 : hi - 1], ALU.mult, ALU.add)
+            nc.vector.scalar_tensor_tensor(quad[:, c0:c1], pair[:, PAD + c0 : hi], 2.0, pair[:, PAD + c0 - 2 : hi - 2], ALU.mult, ALU.add)
+            nc.vector.scalar_tensor_tensor(smo10[:, c0:c1], en[:, PAD + c0 - 1 : hi - 1], 0.5, quad[:, c0:c1], ALU.add, ALU.add)
+
+        logs = sb.tile([P, S], F32, name="logs")
+        nc.scalar.activation(out=logs[:], in_=smo10[:], func=ACT.Ln, scale=0.1)
+        gain = sb.tile([P, S], F32, name="gain")
+        nc.scalar.activation(out=gain[:], in_=logs[:], func=ACT.Exp, scale=alpha_col[:])
+        agc = sb.tile([P, S], F32, name="agc")
+        nc.vector.tensor_tensor(agc[:], gain[:], en[:, PAD:], ALU.mult)
+        res = sb.tile([P, S], F32, name="res")
+        for c0 in range(0, S, OUT_CHUNK):
+            c1 = c0 + OUT_CHUNK
+            nc.scalar.activation(out=res[:, c0:c1], in_=agc[:, c0:c1], func=ACT.Sqrt, bias=2.0)
+            nc.sync.dma_start(out[:, c0:c1], res[:, c0:c1])

@@ -17,7 +17,7 @@ ALU = mybir.AluOpType
 
 P = 128
 PAD = 8
-CHUNK = 256
+CHUNK = 128
 OUT_CHUNK = 256
 
 
@@ -27,20 +27,22 @@ def tile_picked_ypcen_root_p_kernel(tc, x_words, x_scales, w1, alpha, offs, out)
         sb = ctx.enter_context(tc.tile_pool(name="sb", bufs=1))
         ps = ctx.enter_context(tc.psum_pool(name="ps", bufs=1))
 
+        w_raw = sb.tile([P, 4, N], F32, name="w_raw")
+        nc.sync.dma_start(w_raw[:], w1.rearrange("(p j) m -> p j m", j=4))
+        alpha_col = sb.tile([P, 1], F32, name="alpha_col")
+        nc.scalar.dma_start(alpha_col[:], alpha)
         offsets = sb.tile([P, S // 16], U16, name="offsets")
         nc.sync.dma_start(offsets[:], offs)
+        scale_rows = sb.tile([P, T], U8, name="scale_rows", align_bytes=64)
+        for q, queue in enumerate((nc.scalar, nc.sync, nc.scalar, nc.sync)):
+            queue.dma_start(scale_rows[32 * q : 32 * q + 4, :].bitcast(I32), x_scales[0, 4 * q : 4 * q + 4, :].bitcast(I32))
+        word_table = sb.tile([P, T], U32, name="word_table", align_bytes=64)
+        nc.sync.dma_start(word_table[:].bitcast(I32), x_words[0].rearrange("p c r -> p (c r)").bitcast(I32))
 
         scale_table = sb.tile([P, T], U8, name="scale_table", align_bytes=64)
         nc.vector.memset(scale_table[:].bitcast(I32), 0)
-        for r in range(4):
-            nc.scalar.dma_start(scale_table[r:P:32, :].bitcast(I32), x_scales[0, r:16:4, :].bitcast(I32))
-
-        w_raw = sb.tile([P, 4, N], F32, name="w_raw")
-        nc.sync.dma_start(w_raw[:], w1.rearrange("(p j) m -> p j m", j=4))
-        word_table = sb.tile([P, T], U32, name="word_table", align_bytes=64)
-        nc.sync.dma_start(word_table[:].bitcast(I32), x_words[0].rearrange("p c r -> p (c r)").bitcast(I32))
-        alpha_col = sb.tile([P, 1], F32, name="alpha_col")
-        nc.scalar.dma_start(alpha_col[:], alpha)
+        for q in range(4):
+            nc.vector.tensor_copy(scale_table[32 * q : 32 * q + 4, :].bitcast(I32), scale_rows[32 * q : 32 * q + 4, :].bitcast(I32))
 
         w_bf = sb.tile([P, N, 4], BF16, name="w_bf", align_bytes=64)
         nc.scalar.activation(out=w_bf[:], in_=w_raw[:].rearrange("p j m -> p m j"), func=ACT.Copy)
@@ -79,7 +81,7 @@ def tile_picked_ypcen_root_p_kernel(tc, x_words, x_scales, w1, alpha, offs, out)
         agc = sb.tile([P, S], F32, name="agc")
         nc.vector.tensor_tensor(agc[:], gain[:], en[:, PAD:], ALU.mult)
         res = sb.tile([P, S], F32, name="res")
-        for c0 in range(0, S, OUT_CHUNK):
+        for c0, queue in ((0, nc.sync), (OUT_CHUNK, nc.scalar)):
             c1 = c0 + OUT_CHUNK
             nc.scalar.activation(out=res[:, c0:c1], in_=agc[:, c0:c1], func=ACT.Sqrt, bias=2.0)
-            nc.sync.dma_start(out[:, c0:c1], res[:, c0:c1])
+            queue.dma_start(out[:, c0:c1], res[:, c0:c1])

@@ -18,7 +18,6 @@ ALU = mybir.AluOpType
 P = 128
 PAD = 8
 CHUNK = 128
-OUT_CHUNK = 256
 
 
 def tile_picked_ypcen_root_p_kernel(tc, x_words, x_scales, w1, alpha, offs, out):
@@ -27,15 +26,15 @@ def tile_picked_ypcen_root_p_kernel(tc, x_words, x_scales, w1, alpha, offs, out)
         sb = ctx.enter_context(tc.tile_pool(name="sb", bufs=1))
         ps = ctx.enter_context(tc.psum_pool(name="ps", bufs=1))
 
-        w_raw = sb.tile([P, 4, N], F32, name="w_raw")
-        nc.sync.dma_start(w_raw[:], w1.rearrange("(p j) m -> p j m", j=4))
-        alpha_col = sb.tile([P, 1], F32, name="alpha_col")
-        nc.scalar.dma_start(alpha_col[:], alpha)
-        offsets = sb.tile([P, S // 16], U16, name="offsets")
-        nc.sync.dma_start(offsets[:], offs)
         scale_rows = sb.tile([P, T], U8, name="scale_rows", align_bytes=64)
         for q, queue in enumerate((nc.scalar, nc.sync, nc.scalar, nc.sync)):
             queue.dma_start(scale_rows[32 * q : 32 * q + 4, :].bitcast(I32), x_scales[0, 4 * q : 4 * q + 4, :].bitcast(I32))
+        w_raw = sb.tile([P, 4, N], F32, name="w_raw")
+        nc.sync.dma_start(w_raw[:], w1.rearrange("(p j) m -> p j m", j=4))
+        offsets = sb.tile([P, S // 16], U16, name="offsets")
+        nc.sync.dma_start(offsets[:], offs)
+        alpha_col = sb.tile([P, 1], F32, name="alpha_col")
+        nc.scalar.dma_start(alpha_col[:], alpha)
         word_table = sb.tile([P, T], U32, name="word_table", align_bytes=64)
         nc.sync.dma_start(word_table[:].bitcast(I32), x_words[0].rearrange("p c r -> p (c r)").bitcast(I32))
 
@@ -43,6 +42,8 @@ def tile_picked_ypcen_root_p_kernel(tc, x_words, x_scales, w1, alpha, offs, out)
         nc.vector.memset(scale_table[:].bitcast(I32), 0)
         for q in range(4):
             nc.vector.tensor_copy(scale_table[32 * q : 32 * q + 4, :].bitcast(I32), scale_rows[32 * q : 32 * q + 4, :].bitcast(I32))
+        x_sc = sb.tile([P, S], U8, name="x_sc", align_bytes=64)
+        nc.vector.tensor_copy(x_sc[:], scale_table[:].indirect(offsets[:]))
 
         w_bf = sb.tile([P, N, 4], BF16, name="w_bf", align_bytes=64)
         nc.scalar.activation(out=w_bf[:], in_=w_raw[:].rearrange("p j m -> p m j"), func=ACT.Copy)
@@ -50,13 +51,11 @@ def tile_picked_ypcen_root_p_kernel(tc, x_words, x_scales, w1, alpha, offs, out)
         w_scales = sb.tile([P, N], U8, name="w_scales", align_bytes=64)
         nc.vector.quantize_mx(out=w_codes[:].bitcast(FP8X4), scales=w_scales[:], in_=w_bf[:].rearrange("p m j -> p (m j)"))
 
-        x_sc = sb.tile([P, S], U8, name="x_sc", align_bytes=64)
-        nc.vector.tensor_copy(x_sc[:], scale_table[:].indirect(offsets[:]))
 
         en = sb.tile([P, PAD + S], F32, name="en")
         nc.vector.memset(en[:, 0:PAD], 0.0)
-        pair = sb.tile([P, PAD + S], F32, name="pair")
-        quad = sb.tile([P, S], F32, name="quad")
+        near = sb.tile([P, S], F32, name="near")
+        far = sb.tile([P, S], F32, name="far")
         smo10 = sb.tile([P, S], F32, name="smo10")
         x_codes = sb.tile([P, S], U32, name="x_codes", align_bytes=64)
         for c0 in range(0, S, CHUNK):
@@ -68,20 +67,18 @@ def tile_picked_ypcen_root_p_kernel(tc, x_words, x_scales, w1, alpha, offs, out)
             nc.scalar.activation(out=en[:, PAD + c0 : PAD + c1], in_=y[:], func=ACT.Exp)
         for c0 in range(0, S, CHUNK):
             c1 = c0 + CHUNK
-            lo = PAD + c0 - (2 if c0 == 0 else 0)
-            hi = PAD + c1
-            nc.vector.scalar_tensor_tensor(pair[:, lo:hi], en[:, lo:hi], 2.0, en[:, lo - 1 : hi - 1], ALU.mult, ALU.add)
-            nc.vector.scalar_tensor_tensor(quad[:, c0:c1], pair[:, PAD + c0 : hi], 2.0, pair[:, PAD + c0 - 2 : hi - 2], ALU.mult, ALU.add)
-            nc.vector.scalar_tensor_tensor(smo10[:, c0:c1], en[:, PAD + c0 - 1 : hi - 1], 0.5, quad[:, c0:c1], ALU.add, ALU.add)
+            lo, hi = PAD + c0, PAD + c1
+            nc.vector.scalar_tensor_tensor(near[:, c0:c1], en[:, lo:hi], 4.0 / 3.0, en[:, lo - 1 : hi - 1], ALU.mult, ALU.add)
+            nc.vector.scalar_tensor_tensor(far[:, c0:c1], en[:, lo - 2 : hi - 2], 2.0, en[:, lo - 3 : hi - 3], ALU.mult, ALU.add)
+            nc.vector.scalar_tensor_tensor(smo10[:, c0:c1], near[:, c0:c1], 3.0, far[:, c0:c1], ALU.mult, ALU.add)
 
         logs = sb.tile([P, S], F32, name="logs")
-        nc.scalar.activation(out=logs[:], in_=smo10[:], func=ACT.Ln, scale=0.1)
+        nc.scalar.activation(out=logs[:], in_=smo10[:], func=ACT.Ln, scale=0.1, bias=0.05)
         gain = sb.tile([P, S], F32, name="gain")
         nc.scalar.activation(out=gain[:], in_=logs[:], func=ACT.Exp, scale=alpha_col[:])
         agc = sb.tile([P, S], F32, name="agc")
         nc.vector.tensor_tensor(agc[:], gain[:], en[:, PAD:], ALU.mult)
         res = sb.tile([P, S], F32, name="res")
-        for c0, queue in ((0, nc.sync), (OUT_CHUNK, nc.scalar)):
-            c1 = c0 + OUT_CHUNK
+        for c0, c1, queue in ((0, 256, nc.sync), (256, 384, nc.sync), (384, 512, nc.scalar)):
             nc.scalar.activation(out=res[:, c0:c1], in_=agc[:, c0:c1], func=ACT.Sqrt, bias=2.0)
             queue.dma_start(out[:, c0:c1], res[:, c0:c1])

from contextlib import ExitStack

import concourse.mybir as mybir

K, T, S, N = 512, 2048, 512, 128
FLOPS = 2 * K * S * N

F32 = mybir.dt.float32
BF16 = mybir.dt.bfloat16
I32 = mybir.dt.int32
U32 = mybir.dt.uint32
U16 = mybir.dt.uint16
U8 = mybir.dt.uint8
FP8X4 = mybir.dt.float8_e4m3fn_x4
ACT = mybir.ActivationFunctionType
ALU = mybir.AluOpType

P = 128
PAD = 8
CHUNK = 128


def tile_picked_ypcen_root_p_kernel(tc, x_words, x_scales, w1, alpha, offs, out):
    nc = tc.nc
    with ExitStack() as ctx:
        sb = ctx.enter_context(tc.tile_pool(name="sb", bufs=1))
        ps = ctx.enter_context(tc.psum_pool(name="ps", bufs=1))

        scale_rows = sb.tile([P, T], U8, name="scale_rows", align_bytes=64)
        for q, queue in enumerate((nc.scalar, nc.sync, nc.scalar, nc.sync)):
            queue.dma_start(scale_rows[32 * q : 32 * q + 4, :].bitcast(I32), x_scales[0, 4 * q : 4 * q + 4, :].bitcast(I32))
        w_raw = sb.tile([P, 4, N], F32, name="w_raw")
        nc.sync.dma_start(w_raw[:], w1.rearrange("(p j) m -> p j m", j=4))
        offsets = sb.tile([P, S // 16], U16, name="offsets")
        nc.sync.dma_start(offsets[:], offs)
        alpha_col = sb.tile([P, 1], F32, name="alpha_col")
        nc.scalar.dma_start(alpha_col[:], alpha)
        word_table = sb.tile([P, T], U32, name="word_table", align_bytes=64)
        nc.sync.dma_start(word_table[:].bitcast(I32), x_words[0].rearrange("p c r -> p (c r)").bitcast(I32))

        scale_table = sb.tile([P, T], U8, name="scale_table", align_bytes=64)
        nc.vector.memset(scale_table[:].bitcast(I32), 0)
        for q in range(4):
            nc.vector.tensor_copy(scale_table[32 * q : 32 * q + 4, :].bitcast(I32), scale_rows[32 * q : 32 * q + 4, :].bitcast(I32))
        x_sc = sb.tile([P, S], U8, name="x_sc", align_bytes=64)
        nc.vector.tensor_copy(x_sc[:], scale_table[:].indirect(offsets[:]))

        w_bf = sb.tile([P, N, 4], BF16, name="w_bf", align_bytes=64)
        nc.scalar.activation(out=w_bf[:], in_=w_raw[:].rearrange("p j m -> p m j"), func=ACT.Copy)
        w_codes = sb.tile([P, N], U32, name="w_codes", align_bytes=64)
        w_scales = sb.tile([P, N], U8, name="w_scales", align_bytes=64)
        nc.vector.quantize_mx(out=w_codes[:].bitcast(FP8X4), scales=w_scales[:], in_=w_bf[:].rearrange("p m j -> p (m j)"))


        en = sb.tile([P, PAD + S], F32, name="en")
        nc.vector.memset(en[:, 0:PAD], 0.0)
        near = sb.tile([P, S], F32, name="near")
        far = sb.tile([P, S], F32, name="far")
        smo10 = sb.tile([P, S], F32, name="smo10")
        x_codes = sb.tile([P, S], U32, name="x_codes", align_bytes=64)
        for c0 in range(0, S, CHUNK):
            c1 = c0 + CHUNK
            nc.vector.tensor_copy(x_codes[:, c0:c1], word_table[:].indirect(offsets[:, c0 // 16 : c1 // 16]))
            y = ps.tile([P, CHUNK], F32, name="y%d" % c0)
            nc.tensor.matmul_mx(out=y[:], lhsT=w_codes[:].bitcast(FP8X4), lhsT_scale=w_scales[:],
                                rhs=x_codes[:, c0:c1].bitcast(FP8X4), rhs_scale=x_sc[:, c0:c1], start=True, stop=True)
            nc.scalar.activation(out=en[:, PAD + c0 : PAD + c1], in_=y[:], func=ACT.Exp)
        for c0 in range(0, S, CHUNK):
            c1 = c0 + CHUNK
            lo, hi = PAD + c0, PAD + c1
            nc.vector.scalar_tensor_tensor(near[:, c0:c1], en[:, lo:hi], 4.0 / 3.0, en[:, lo - 1 : hi - 1], ALU.mult, ALU.add)
            nc.vector.scalar_tensor_tensor(far[:, c0:c1], en[:, lo - 2 : hi - 2], 2.0, en[:, lo - 3 : hi - 3], ALU.mult, ALU.add)
            nc.vector.scalar_tensor_tensor(smo10[:, c0:c1], near[:, c0:c1], 3.0, far[:, c0:c1], ALU.mult, ALU.add)

        logs = sb.tile([P, S], F32, name="logs")
        nc.scalar.activation(out=logs[:], in_=smo10[:], func=ACT.Ln, scale=0.1, bias=0.05)
        gain = sb.tile([P, S], F32, name="gain")
        nc.scalar.activation(out=gain[:], in_=logs[:], func=ACT.Exp, scale=alpha_col[:])
        agc = sb.tile([P, S], F32, name="agc")
        nc.vector.tensor_tensor(agc[:], gain[:], en[:, PAD:], ALU.mult)
        res = sb.tile([P, S], F32, name="res")
        for c0, c1, queue in ((0, 256, nc.sync), (256, 384, nc.sync), (384, 512, nc.scalar)):
            nc.scalar.activation(out=res[:, c0:c1], in_=agc[:, c0:c1], func=ACT.Sqrt, bias=2.0)
            queue.dma_start(out[:, c0:c1], res[:, c0:c1])
